import numpy as np
import ml_dtypes


def mxq(x, axis, fmt="e4m3"):
    dtype, down = {"e4m3": (ml_dtypes.float8_e4m3fn, 7), "e5m2": (ml_dtypes.float8_e5m2, 14)}[fmt]
    v = np.moveaxis(np.asarray(x, np.float32).astype(ml_dtypes.bfloat16).astype(np.float64), axis, -1)
    blocks = v.reshape(v.shape[:-1] + (-1, 32))
    amax = np.abs(blocks).max(-1, keepdims=True)
    byte = np.maximum(np.where(amax > 0, np.frexp(amax)[1] - 1 + 127, 0) - down, 1)
    scale = np.exp2(byte - 127.0)
    codes = (blocks / scale).astype(np.float32).astype(dtype).astype(np.float64)
    return np.moveaxis((codes * scale).reshape(v.shape), -1, axis)


WIDE = False


def mx_kscale(k):
    if not WIDE:
        return np.ones(k)
    levels = np.array([30, -30])
    if k % 512:
        return np.exp2(np.random.permutation(np.resize(levels, k // 32))).repeat(32)
    a = np.empty((k // 512, 16))
    for p in range(k // 512):
        a[p, :8] = np.random.permutation(np.resize(levels, 8))
        for g in range(8):
            far = levels[np.abs(levels - a[p, g]) >= 10]
            a[p, g + 8] = far[np.random.randint(len(far))]
    return np.exp2(a.ravel()).repeat(32)


def f64(x):
    return np.asarray(x).astype(np.float64)


def striped(idx):
    return np.tile(np.asarray(idx).reshape(-1, 16).T, (8, 1)).astype(np.uint16)


def unstriped(offs):
    return offs[:16].T.reshape(-1).astype(np.int64)


E2M1 = np.array([0.0, 0.5, 1.0, 1.5, 2.0, 3.0, 4.0, 6.0, -0.0, -0.5, -1.0, -1.5, -2.0, -3.0, -4.0, -6.0])


def pack_weight(w, fmt):
    k, n = w.shape
    w = f64(np.asarray(w, np.float32).astype(ml_dtypes.bfloat16)).reshape(k // 32, 32, n)
    amax = np.abs(w).max(1)
    if fmt in ("e4m3", "e5m2"):
        byte = np.frexp(amax)[1] - 1 + 127 - (7 if fmt == "e4m3" else 14)
    else:
        mant, ex = np.frexp(amax / 6.0)
        byte = np.where(mant > 0.5, ex, ex - 1) + 127
    byte = np.clip(np.where(amax > 0, byte, 1), 1, 254)
    scaled = (w * np.exp2(127.0 - byte)[:, None, :]).reshape(k, n).astype(np.float32)
    by_word = np.ascontiguousarray(scaled.reshape(k // 512, 128, 4, n).transpose(0, 1, 3, 2))
    if fmt in ("e4m3", "e5m2"):
        words = by_word.astype(ml_dtypes.float8_e4m3fn if fmt == "e4m3" else ml_dtypes.float8_e5m2).view(np.uint8)
    else:
        c = by_word.astype(ml_dtypes.float4_e2m1fn).view(np.uint8) & 0xF
        words = (c[..., 0::2] | (c[..., 1::2] << 4)).reshape(k // 512, 128, 2 * n)
    return np.ascontiguousarray(words), np.ascontiguousarray(byte.astype(np.uint8).reshape(k // 512, 16, n))


def unpack_weight(words, scales, fmt):
    g, _, n = scales.shape
    words = np.ascontiguousarray(words).reshape(g, 128, n, -1)
    if fmt in ("e4m3", "e5m2"):
        vals = words.view(ml_dtypes.float8_e4m3fn if fmt == "e4m3" else ml_dtypes.float8_e5m2).astype(np.float64)
    else:
        nib = np.empty((g, 128, n, 4), np.uint8)
        nib[..., 0::2] = words & 0xF
        nib[..., 1::2] = words >> 4
        vals = E2M1[nib]
    vals = vals * np.repeat(np.exp2(scales.astype(np.float64) - 127.0), 8, axis=1)[..., None]
    return vals.transpose(0, 1, 3, 2).reshape(g * 512, n)


K, T, J, R, F, Z, O, U, D, N, E = 512, 1024, 256, 512, 512, 1024, 128, 128, 256, 256, 1024


def setup_inputs():
    n = np.random.standard_normal
    idx = np.random.permutation(T)[:J]
    idx2 = np.random.permutation(Z)[:J]
    idx3 = np.random.permutation(J)[:O]
    idx4 = np.random.permutation(J)[:U]
    idx5 = np.random.permutation(T)[:D]
    idx6 = np.random.permutation(E)[:D]
    fk = mx_kscale(K)
    ff = mx_kscale(F)
    fr = mx_kscale(R)
    xtp = pack_weight(n((K, T)) / fk[:, None], "e4m3")
    xop = pack_weight(n((F, Z)) / ff[:, None], "e2m1")
    wp = pack_weight(n((K, R)) * 1 / np.sqrt(K) * fk[:, None] * fr, "e2m1")
    w2p = pack_weight(n((F, R)) * 1 / np.sqrt(F) * ff[:, None], "e5m2")
    wbp = pack_weight(n((R, N)) * 1 / np.sqrt(R) / fr[:, None], "e5m2")
    wsp = pack_weight(n((K, N)) * 1 / np.sqrt(K) * fk[:, None], "e5m2")
    return {
        "xt_words": xtp[0],
        "xt_scales": xtp[1],
        "xo_words": xop[0],
        "xo_scales": xop[1],
        "w_words": wp[0],
        "w_scales": wp[1],
        "w2_words": w2p[0],
        "w2_scales": w2p[1],
        "wb_words": wbp[0],
        "wb_scales": wbp[1],
        "ws_words": wsp[0],
        "ws_scales": wsp[1],
        "offs": striped(idx),
        "offs2": striped(idx2),
        "offs3": striped(idx3),
        "offs4": striped(idx4),
        "offs5": striped(idx5),
        "offs6": striped(idx6),
    }


def reference(xt_words, xt_scales, xo_words, xo_scales, w_words, w_scales, w2_words, w2_scales, wb_words, wb_scales, ws_words, ws_scales, offs, offs2, offs3, offs4, offs5, offs6):
    idx = unstriped(offs)
    idx2 = unstriped(offs2)
    idx3 = unstriped(offs3)
    idx4 = unstriped(offs4)
    idx5 = unstriped(offs5)
    idx6 = unstriped(offs6)
    xtu = unpack_weight(xt_words, xt_scales, "e4m3")
    xou = unpack_weight(xo_words, xo_scales, "e2m1")
    wu = unpack_weight(w_words, w_scales, "e2m1")
    w2u = unpack_weight(w2_words, w2_scales, "e5m2")
    wbu = unpack_weight(wb_words, wb_scales, "e5m2")
    wsu = unpack_weight(ws_words, ws_scales, "e5m2")
    xtidxg = xtu[:, idx]
    a = wu.T @ xtidxg
    xoidx2g = xou[:, idx2]
    b = w2u.T @ xoidx2g
    lb = b[:, 0:1]
    la = a[:, 0:1]
    h1 = a[:, idx3] * lb
    h2 = b[:, idx4] * la
    hid = np.concatenate([h1, h2], axis=1)
    hidq = mxq(hid, 0, "e4m3")
    xtidx5g = xtu[:, idx5]
    p = wbu.T @ hidq + wsu.T @ xtidx5g
    y = np.zeros((N, E))
    y[:, idx6] = p
    return y

@@ -1,0 +1,175 @@
+from contextlib import ExitStack
+
+import concourse.mybir as mybir
+
+K, T, J, R, Z, D, N, E = 512, 1024, 256, 512, 1024, 256, 256, 1024
+FLOPS = 2 * (K * R * J + K * R * J + R * N * D + K * N * D)
+
+F32 = mybir.dt.float32
+BF16 = mybir.dt.bfloat16
+I32 = mybir.dt.int32
+U32 = mybir.dt.uint32
+U16 = mybir.dt.uint16
+U8 = mybir.dt.uint8
+E4M3 = mybir.dt.float8_e4m3fn_x4
+E5M2 = mybir.dt.float8_e5m2_x4
+E2M1 = mybir.dt.float4_e2m1fn_x4
+COPY = mybir.ActivationFunctionType.Copy
+
+P = 128
+PACK = 4
+HALF = 128
+LIST_COLS = HALF // 16
+
+
+def tile_list_sidebyside_twotab_further_scattered_kernel(
+    tc, xt_words, xt_scales, xo_words, xo_scales, w_words, w_scales, w2_words, w2_scales,
+    wb_words, wb_scales, ws_words, ws_scales, offs, offs2, offs3, offs4, offs5, offs6, out,
+):
+    nc = tc.nc
+    with ExitStack() as ctx:
+        sb = ctx.enter_context(tc.tile_pool(name="sb", bufs=1))
+        ps = ctx.enter_context(tc.psum_pool(name="ps", bufs=1))
+
+        def sbuf(name, shape, dtype):
+            return sb.tile(shape, dtype, name=name, align_bytes=64)
+
+        def load_list(name, src):
+            tile = sbuf(name, list(src.shape), U16)
+            nc.sync.dma_start(tile[:], src)
+            return tile
+
+        def load_words(queue, name, src, columns, dtype):
+            tile = sbuf(name, [P, columns], dtype)
+            rows = src[0] if src.ndim == 3 else src[0].rearrange("p c t -> p (c t)")
+            queue.dma_start(tile[:].bitcast(I32), rows.bitcast(I32))
+            return tile
+
+        def zeroed_plane(name, columns):
+            tile = sbuf(name, [P, columns], U8)
+            nc.vector.memset(tile[:].bitcast(I32), 0)
+            return tile
+
+        def load_plane(queue, tile, src):
+            for q in range(4):
+                queue.dma_start(tile[32 * q : 32 * q + 4, :].bitcast(I32), src[0, 4 * q : 4 * q + 4, :].bitcast(I32))
+
+        def dealt(view):
+            return view.rearrange("p (m t) -> p t m", t=PACK)
+
+        xo_plane = zeroed_plane("xo_plane", Z)
+        w2_plane = zeroed_plane("w2_plane", R)
+        xt_plane = zeroed_plane("xt_plane", T)
+        w_plane = zeroed_plane("w_plane", R)
+        ws_plane = zeroed_plane("ws_plane", N)
+        wb_plane = zeroed_plane("wb_plane", N)
+
+        list2 = load_list("list2", offs2)
+        xo_table = load_words(nc.sync, "xo_table", xo_words, Z, U16)
+        w2_raw = load_words(nc.scalar, "w2_raw", w2_words, R, U32)
+        xt_table = load_words(nc.scalar, "xt_table", xt_words, T, U32)
+        load_plane(nc.sync, xo_plane, xo_scales)
+        load_plane(nc.sync, w2_plane, w2_scales)
+        list1 = load_list("list1", offs)
+        w_raw = load_words(nc.sync, "w_raw", w_words, R, U16)
+        load_plane(nc.sync, xt_plane, xt_scales)
+        load_plane(nc.sync, w_plane, w_scales)
+        list4 = load_list("list4", offs4)
+        list3 = load_list("list3", offs3)
+        list5 = load_list("list5", offs5)
+        ws_codes = load_words(nc.sync, "ws_codes", ws_words, N, U32)
+        load_plane(nc.sync, ws_plane, ws_scales)
+        wb_codes = load_words(nc.sync, "wb_codes", wb_words, N, U32)
+        load_plane(nc.sync, wb_plane, wb_scales)
+        list6 = load_list("list6", offs6)
+
+        pages = [sbuf("page%d" % n, [P, E], F32) for n in range(N // P)]
+        for page in pages:
+            nc.vector.memset(page[:], 0.0)
+
+        def halves(h):
+            return slice(h * HALF, (h + 1) * HALF), slice(h * LIST_COLS, (h + 1) * LIST_COLS)
+
+        xo_codes = sbuf("xo_codes", [P, J], U16)
+        xo_bytes = sbuf("xo_bytes", [P, J], U8)
+        nc.vector.tensor_copy(xo_codes[:], xo_table[:].indirect(list2[:]))
+        nc.vector.tensor_copy(xo_bytes[:], xo_plane[:].indirect(list2[:]))
+        w2_codes = sbuf("w2_codes", [P, PACK, P], U32)
+        w2_bytes = sbuf("w2_bytes", [P, PACK, P], U8)
+        nc.scalar.copy(w2_codes[:], dealt(w2_raw[:]))
+        nc.vector.tensor_copy(w2_bytes[:], dealt(w2_plane[:]))
+        w_codes = sbuf("w_codes", [P, PACK, P], U16)
+        w_bytes = sbuf("w_bytes", [P, PACK, P], U8)
+        nc.scalar.copy(w_codes[:], dealt(w_raw[:]))
+
+        b_rows = []
+        for t in range(PACK):
+            bank = ps.tile([P, J], F32, name="b_bank%d" % t, tag="wide%d" % t)
+            nc.tensor.matmul_mx(
+                out=bank[:], lhsT=w2_codes[:, t, :].bitcast(E5M2), lhsT_scale=w2_bytes[:, t, :],
+                rhs=xo_codes[:].bitcast(E2M1), rhs_scale=xo_bytes[:], start=True, stop=True,
+            )
+            rows = sbuf("b_rows%d" % t, [P, J], F32)
+            nc.scalar.copy(rows[:], bank[:])
+            b_rows.append(rows)
+
+        nc.vector.tensor_copy(w_bytes[:], dealt(w_plane[:]))
+        xt_codes = sbuf("xt_codes", [P, J], U32)
+        xt_bytes = sbuf("xt_bytes", [P, J], U8)
+        a_rows = [sbuf("a_rows%d" % t, [P, J], F32) for t in range(PACK)]
+        a_banks = []
+        for h in range(J // HALF):
+            cols, entries = halves(h)
+            nc.vector.tensor_copy(xt_codes[:, cols], xt_table[:].indirect(list1[:, entries]))
+            nc.vector.tensor_copy(xt_bytes[:, cols], xt_plane[:].indirect(list1[:, entries]))
+            bank = ps.tile([P, PACK, HALF], F32, name="a_bank%d" % h)
+            for t in range(PACK):
+                nc.tensor.matmul_mx(
+                    out=bank[:, t, :], lhsT=w_codes[:, t, :].bitcast(E2M1), lhsT_scale=w_bytes[:, t, :],
+                    rhs=xt_codes[:, cols].bitcast(E4M3), rhs_scale=xt_bytes[:, cols], start=True, stop=True,
+                )
+            a_banks.append(bank)
+        for h in range(J // HALF):
+            for t in range(PACK):
+                nc.vector.tensor_copy(a_rows[t][:, halves(h)[0]], a_banks[h][:, t, :])
+
+        short_codes = sbuf("short_codes", [P, D], U32)
+        short_bytes = sbuf("short_bytes", [P, D], U8)
+        picks = {1: (b_rows, list4, a_rows), 0: (a_rows, list3, b_rows)}
+        for step, h in enumerate((1, 0)):
+            cols, entries = halves(h)
+            source, places, other = picks[h]
+            picked = sbuf("picked%d" % h, [P, PACK, HALF], BF16)
+            for t in range(PACK):
+                nc.scalar.activation(picked[:, t, :], source[t][:].indirect(places[:]), COPY, scale=other[t][:, 0:1])
+            nc.vector.tensor_copy(short_codes[:, cols], xt_table[:].indirect(list5[:, entries]))
+            nc.vector.tensor_copy(short_bytes[:, cols], xt_plane[:].indirect(list5[:, entries]))
+            woven = sbuf("woven%d" % h, [P, HALF, PACK], BF16)
+            nc.vector.tensor_copy(woven[:], picked[:].rearrange("p t c -> p c t"))
+            hid_codes = sbuf("hid_codes%d" % h, [P, HALF], U32)
+            hid_bytes = sbuf("hid_bytes%d" % h, [P, HALF], U8)
+            nc.vector.quantize_mx(
+                out=hid_codes[:].bitcast(E4M3), scales=hid_bytes[:], in_=woven[:].rearrange("p c t -> p (c t)")
+            )
+            for n in range(N // P):
+                rows = slice(n * P, (n + 1) * P)
+                bank = ps.tile([P, HALF], F32, name="p_bank%d_%d" % (h, n), tag="wide%d" % (2 * step + n))
+                nc.tensor.matmul_mx(
+                    out=bank[:], lhsT=ws_codes[:, rows].bitcast(E5M2), lhsT_scale=ws_plane[:, rows],
+                    rhs=short_codes[:, cols].bitcast(E4M3), rhs_scale=short_bytes[:, cols], start=True, stop=False,
+                )
+                nc.tensor.matmul_mx(
+                    out=bank[:], lhsT=wb_codes[:, rows].bitcast(E5M2), lhsT_scale=wb_plane[:, rows],
+                    rhs=hid_codes[:].bitcast(E4M3), rhs_scale=hid_bytes[:], start=False, stop=True,
+                )
+                sums = sbuf("sums%d_%d" % (h, n), [P, HALF], F32)
+                target = pages[n][:].indirect(list6[:, entries])
+                if n == 0:
+                    nc.scalar.copy(sums[:], bank[:])
+                    nc.scalar.activation(target, sums[:], COPY)
+                else:
+                    nc.vector.tensor_copy(sums[:], bank[:])
+                    nc.vector.tensor_copy(target, sums[:])
+
+        nc.scalar.dma_start(out[0:P, :], pages[0][:])
+        nc.sync.dma_start(out[P : 2 * P, :], pages[1][:])

@@ -18,8 +18,13 @@ COPY = mybir.ActivationFunctionType.Copy
 
 P = 128
 PACK = 4
+QUADRANT = 32
+QUADRANTS = P // QUADRANT
+LIVE = 4
 HALF = 128
 LIST_COLS = HALF // 16
+LINE = 16
+ROW_WORDS = R // 4
 
 
 def tile_list_sidebyside_twotab_further_scattered_kernel(
@@ -39,10 +44,10 @@ def tile_list_sidebyside_twotab_further_scattered_kernel(
             nc.sync.dma_start(tile[:], src)
             return tile
 
-        def load_words(queue, name, src, columns, dtype):
+        def load_words(name, src, columns, dtype):
             tile = sbuf(name, [P, columns], dtype)
             rows = src[0] if src.ndim == 3 else src[0].rearrange("p c t -> p (c t)")
-            queue.dma_start(tile[:].bitcast(I32), rows.bitcast(I32))
+            nc.sync.dma_start(tile[:].bitcast(I32), rows.bitcast(I32))
             return tile
 
         def zeroed_plane(name, columns):
@@ -50,61 +55,85 @@ def tile_list_sidebyside_twotab_further_scattered_kernel(
             nc.vector.memset(tile[:].bitcast(I32), 0)
             return tile
 
-        def load_plane(queue, tile, src):
-            for q in range(4):
-                queue.dma_start(tile[32 * q : 32 * q + 4, :].bitcast(I32), src[0, 4 * q : 4 * q + 4, :].bitcast(I32))
+        def load_plane(plane, src):
+            for q in range(QUADRANTS):
+                nc.sync.dma_start(
+                    plane[QUADRANT * q : QUADRANT * q + LIVE, :].bitcast(I32),
+                    src[0, LIVE * q : LIVE * (q + 1), :].bitcast(I32),
+                )
 
-        def dealt(view):
-            return view.rearrange("p (m t) -> p t m", t=PACK)
+        def zeroed_folded(name):
+            tile = sbuf(name, [P, 2 * ROW_WORDS], I32)
+            nc.vector.memset(tile[0 : P // 2, :], 0)
+            return tile
 
+        def load_folded(folded, src):
+            rows = src[0].bitcast(I32).rearrange("(h q s) c -> q s h c", h=2, q=2)
+            for q in range(2):
+                nc.sync.dma_start(
+                    folded[QUADRANT * q : QUADRANT * q + LIVE, :].rearrange("s (h c) -> s h c", h=2), rows[q]
+                )
+
+        def deal(copy, dealt, natural, item_bytes):
+            run = LINE // item_bytes
+            copy(
+                dealt.rearrange("p t (c i) -> p c t i", i=run),
+                natural.rearrange("p (c i t) -> p c t i", i=run, t=PACK),
+            )
+
+        def unfold_and_deal(dealt_bytes, folded):
+            nc.vector.tensor_copy(folded[P // 2 : P, 0:ROW_WORDS], folded[0 : P // 2, ROW_WORDS : 2 * ROW_WORDS])
+            deal(nc.vector.tensor_copy, dealt_bytes[:], folded[:, 0:ROW_WORDS].bitcast(U8), 1)
+
+        def half(h):
+            return slice(h * HALF, (h + 1) * HALF), slice(h * LIST_COLS, (h + 1) * LIST_COLS)
+
+        w2_folded = zeroed_folded("w2_folded")
         xo_plane = zeroed_plane("xo_plane", Z)
-        w2_plane = zeroed_plane("w2_plane", R)
+        w_folded = zeroed_folded("w_folded")
         xt_plane = zeroed_plane("xt_plane", T)
-        w_plane = zeroed_plane("w_plane", R)
-        ws_plane = zeroed_plane("ws_plane", N)
         wb_plane = zeroed_plane("wb_plane", N)
+        ws_plane = zeroed_plane("ws_plane", N)
 
         list2 = load_list("list2", offs2)
-        xo_table = load_words(nc.sync, "xo_table", xo_words, Z, U16)
-        w2_raw = load_words(nc.scalar, "w2_raw", w2_words, R, U32)
-        xt_table = load_words(nc.scalar, "xt_table", xt_words, T, U32)
-        load_plane(nc.sync, xo_plane, xo_scales)
-        load_plane(nc.sync, w2_plane, w2_scales)
+        xo_table = load_words("xo_table", xo_words, Z, U16)
+        load_folded(w2_folded, w2_scales)
+        load_plane(xo_plane, xo_scales)
+        w2_natural = load_words("w2_natural", w2_words, R, U32)
+        load_folded(w_folded, w_scales)
+        w_natural = load_words("w_natural", w_words, R, U16)
+        xt_table = load_words("xt_table", xt_words, T, U32)
+        load_plane(xt_plane, xt_scales)
         list1 = load_list("list1", offs)
-        w_raw = load_words(nc.sync, "w_raw", w_words, R, U16)
-        load_plane(nc.sync, xt_plane, xt_scales)
-        load_plane(nc.sync, w_plane, w_scales)
         list4 = load_list("list4", offs4)
-        list3 = load_list("list3", offs3)
         list5 = load_list("list5", offs5)
-        ws_codes = load_words(nc.sync, "ws_codes", ws_words, N, U32)
-        load_plane(nc.sync, ws_plane, ws_scales)
-        wb_codes = load_words(nc.sync, "wb_codes", wb_words, N, U32)
-        load_plane(nc.sync, wb_plane, wb_scales)
+        list3 = load_list("list3", offs3)
         list6 = load_list("list6", offs6)
+        wb_codes = load_words("wb_codes", wb_words, N, U32)
+        load_plane(wb_plane, wb_scales)
+        ws_codes = load_words("ws_codes", ws_words, N, U32)
+        load_plane(ws_plane, ws_scales)
 
         pages = [sbuf("page%d" % n, [P, E], F32) for n in range(N // P)]
         for page in pages:
             nc.vector.memset(page[:], 0.0)
 
-        def halves(h):
-            return slice(h * HALF, (h + 1) * HALF), slice(h * LIST_COLS, (h + 1) * LIST_COLS)
-
         xo_codes = sbuf("xo_codes", [P, J], U16)
         xo_bytes = sbuf("xo_bytes", [P, J], U8)
-        nc.vector.tensor_copy(xo_codes[:], xo_table[:].indirect(list2[:]))
-        nc.vector.tensor_copy(xo_bytes[:], xo_plane[:].indirect(list2[:]))
         w2_codes = sbuf("w2_codes", [P, PACK, P], U32)
         w2_bytes = sbuf("w2_bytes", [P, PACK, P], U8)
-        nc.scalar.copy(w2_codes[:], dealt(w2_raw[:]))
-        nc.vector.tensor_copy(w2_bytes[:], dealt(w2_plane[:]))
         w_codes = sbuf("w_codes", [P, PACK, P], U16)
         w_bytes = sbuf("w_bytes", [P, PACK, P], U8)
-        nc.scalar.copy(w_codes[:], dealt(w_raw[:]))
+        nc.vector.tensor_copy(xo_codes[:], xo_table[:].indirect(list2[:]))
+        unfold_and_deal(w2_bytes, w2_folded)
+        nc.vector.tensor_copy(xo_bytes[:], xo_plane[:].indirect(list2[:]))
+        unfold_and_deal(w_bytes, w_folded)
+        deal(nc.scalar.copy, w2_codes[:], w2_natural[:], 4)
+        deal(nc.scalar.copy, w_codes[:], w_natural[:], 2)
 
         b_rows = []
         for t in range(PACK):
-            bank = ps.tile([P, J], F32, name="b_bank%d" % t, tag="wide%d" % t)
+            bank = ps.tile([P, J], F32, name="b_bank%d" % t, tag="reused%d" % t)
             nc.tensor.matmul_mx(
                 out=bank[:], lhsT=w2_codes[:, t, :].bitcast(E5M2), lhsT_scale=w2_bytes[:, t, :],
                 rhs=xo_codes[:].bitcast(E2M1), rhs_scale=xo_bytes[:], start=True, stop=True,
@@ -113,62 +142,68 @@ def tile_list_sidebyside_twotab_further_scattered_kernel(
             nc.scalar.copy(rows[:], bank[:])
             b_rows.append(rows)
 
-        nc.vector.tensor_copy(w_bytes[:], dealt(w_plane[:]))
         xt_codes = sbuf("xt_codes", [P, J], U32)
         xt_bytes = sbuf("xt_bytes", [P, J], U8)
         a_rows = [sbuf("a_rows%d" % t, [P, J], F32) for t in range(PACK)]
         a_banks = []
         for h in range(J // HALF):
-            cols, entries = halves(h)
+            cols, entries = half(h)
             nc.vector.tensor_copy(xt_codes[:, cols], xt_table[:].indirect(list1[:, entries]))
             nc.vector.tensor_copy(xt_bytes[:, cols], xt_plane[:].indirect(list1[:, entries]))
-            bank = ps.tile([P, PACK, HALF], F32, name="a_bank%d" % h)
+            banks = [ps.tile([P, 2, HALF], F32, name="a_bank%d_%d" % (h, u)) for u in range(PACK // 2)]
             for t in range(PACK):
                 nc.tensor.matmul_mx(
-                    out=bank[:, t, :], lhsT=w_codes[:, t, :].bitcast(E2M1), lhsT_scale=w_bytes[:, t, :],
+                    out=banks[t // 2][:, t % 2, :], lhsT=w_codes[:, t, :].bitcast(E2M1), lhsT_scale=w_bytes[:, t, :],
                     rhs=xt_codes[:, cols].bitcast(E4M3), rhs_scale=xt_bytes[:, cols], start=True, stop=True,
                 )
-            a_banks.append(bank)
+            a_banks.append(banks)
         for h in range(J // HALF):
             for t in range(PACK):
-                nc.vector.tensor_copy(a_rows[t][:, halves(h)[0]], a_banks[h][:, t, :])
+                nc.vector.tensor_copy(a_rows[t][:, half(h)[0]], a_banks[h][t // 2][:, t % 2, :])
 
         short_codes = sbuf("short_codes", [P, D], U32)
         short_bytes = sbuf("short_bytes", [P, D], U8)
         picks = {1: (b_rows, list4, a_rows), 0: (a_rows, list3, b_rows)}
         for step, h in enumerate((1, 0)):
-            cols, entries = halves(h)
-            source, places, other = picks[h]
+            cols, entries = half(h)
+            source, places, partner = picks[h]
+
             picked = sbuf("picked%d" % h, [P, PACK, HALF], BF16)
             for t in range(PACK):
-                nc.scalar.activation(picked[:, t, :], source[t][:].indirect(places[:]), COPY, scale=other[t][:, 0:1])
+                nc.scalar.activation(picked[:, t, :], source[t][:].indirect(places[:]), COPY, scale=partner[t][:, 0:1])
             nc.vector.tensor_copy(short_codes[:, cols], xt_table[:].indirect(list5[:, entries]))
             nc.vector.tensor_copy(short_bytes[:, cols], xt_plane[:].indirect(list5[:, entries]))
+
             woven = sbuf("woven%d" % h, [P, HALF, PACK], BF16)
-            nc.vector.tensor_copy(woven[:], picked[:].rearrange("p t c -> p c t"))
+            nc.vector.tensor_copy(
+                woven[:].rearrange("p (c i) t -> p c t i", i=4), picked[:].rearrange("p t (c i) -> p c t i", i=4)
+            )
             hid_codes = sbuf("hid_codes%d" % h, [P, HALF], U32)
             hid_bytes = sbuf("hid_bytes%d" % h, [P, HALF], U8)
             nc.vector.quantize_mx(
-                out=hid_codes[:].bitcast(E4M3), scales=hid_bytes[:], in_=woven[:].rearrange("p c t -> p (c t)")
+                out=hid_codes[:].bitcast(E4M3), scales=hid_bytes[:], in_=woven[:].rearrange("p d t -> p (d t)")
             )
-            for n in range(N // P):
-                rows = slice(n * P, (n + 1) * P)
-                bank = ps.tile([P, HALF], F32, name="p_bank%d_%d" % (h, n), tag="wide%d" % (2 * step + n))
+
+            for n in (h, 1 - h):
+                out_rows = slice(n * P, (n + 1) * P)
+                bank = ps.tile([P, HALF], F32, name="p_bank%d_%d" % (h, n), tag="reused%d" % (2 * step + n))
                 nc.tensor.matmul_mx(
-                    out=bank[:], lhsT=ws_codes[:, rows].bitcast(E5M2), lhsT_scale=ws_plane[:, rows],
+                    out=bank[:], lhsT=ws_codes[:, out_rows].bitcast(E5M2), lhsT_scale=ws_plane[:, out_rows],
                     rhs=short_codes[:, cols].bitcast(E4M3), rhs_scale=short_bytes[:, cols], start=True, stop=False,
                 )
                 nc.tensor.matmul_mx(
-                    out=bank[:], lhsT=wb_codes[:, rows].bitcast(E5M2), lhsT_scale=wb_plane[:, rows],
+                    out=bank[:], lhsT=wb_codes[:, out_rows].bitcast(E5M2), lhsT_scale=wb_plane[:, out_rows],
                     rhs=hid_codes[:].bitcast(E4M3), rhs_scale=hid_bytes[:], start=False, stop=True,
                 )
-                sums = sbuf("sums%d_%d" % (h, n), [P, HALF], F32)
                 target = pages[n][:].indirect(list6[:, entries])
                 if n == 0:
+                    sums = sbuf("sums0", [P, HALF], F32)
                     nc.scalar.copy(sums[:], bank[:])
                     nc.scalar.activation(target, sums[:], COPY)
                 else:
-                    nc.vector.tensor_copy(sums[:], bank[:])
+                    sums = sbuf("sums1_%d" % h, [P, HALF], F32)
+                    empty = nc.scalar.copy if step == 0 else nc.vector.tensor_copy
+                    empty(sums[:], bank[:])
                     nc.vector.tensor_copy(target, sums[:])
 
         nc.scalar.dma_start(out[0:P, :], pages[0][:])

from contextlib import ExitStack

import concourse.mybir as mybir

K, T, J, R, Z, D, N, E = 512, 1024, 256, 512, 1024, 256, 256, 1024
FLOPS = 2 * (K * R * J + K * R * J + R * N * D + K * N * D)

F32 = mybir.dt.float32
BF16 = mybir.dt.bfloat16
I32 = mybir.dt.int32
U32 = mybir.dt.uint32
U16 = mybir.dt.uint16
U8 = mybir.dt.uint8
E4M3 = mybir.dt.float8_e4m3fn_x4
E5M2 = mybir.dt.float8_e5m2_x4
E2M1 = mybir.dt.float4_e2m1fn_x4
COPY = mybir.ActivationFunctionType.Copy

P = 128
PACK = 4
QUADRANT = 32
QUADRANTS = P // QUADRANT
LIVE = 4
HALF = 128
LIST_COLS = HALF // 16
LINE = 16
ROW_WORDS = R // 4


def tile_list_sidebyside_twotab_further_scattered_kernel(
    tc, xt_words, xt_scales, xo_words, xo_scales, w_words, w_scales, w2_words, w2_scales,
    wb_words, wb_scales, ws_words, ws_scales, offs, offs2, offs3, offs4, offs5, offs6, out,
):
    nc = tc.nc
    with ExitStack() as ctx:
        sb = ctx.enter_context(tc.tile_pool(name="sb", bufs=1))
        ps = ctx.enter_context(tc.psum_pool(name="ps", bufs=1))

        def sbuf(name, shape, dtype):
            return sb.tile(shape, dtype, name=name, align_bytes=64)

        def load_list(name, src):
            tile = sbuf(name, list(src.shape), U16)
            nc.sync.dma_start(tile[:], src)
            return tile

        def load_words(name, src, columns, dtype):
            tile = sbuf(name, [P, columns], dtype)
            rows = src[0] if src.ndim == 3 else src[0].rearrange("p c t -> p (c t)")
            nc.sync.dma_start(tile[:].bitcast(I32), rows.bitcast(I32))
            return tile

        def zeroed_plane(name, columns):
            tile = sbuf(name, [P, columns], U8)
            nc.vector.memset(tile[:].bitcast(I32), 0)
            return tile

        def load_plane(plane, src):
            for q in range(QUADRANTS):
                nc.sync.dma_start(
                    plane[QUADRANT * q : QUADRANT * q + LIVE, :].bitcast(I32),
                    src[0, LIVE * q : LIVE * (q + 1), :].bitcast(I32),
                )

        def zeroed_folded(name):
            tile = sbuf(name, [P, 2 * ROW_WORDS], I32)
            nc.vector.memset(tile[0 : P // 2, :], 0)
            return tile

        def load_folded(folded, src):
            rows = src[0].bitcast(I32).rearrange("(h q s) c -> q s h c", h=2, q=2)
            for q in range(2):
                nc.sync.dma_start(
                    folded[QUADRANT * q : QUADRANT * q + LIVE, :].rearrange("s (h c) -> s h c", h=2), rows[q]
                )

        def deal(copy, dealt, natural, item_bytes):
            run = LINE // item_bytes
            copy(
                dealt.rearrange("p t (c i) -> p c t i", i=run),
                natural.rearrange("p (c i t) -> p c t i", i=run, t=PACK),
            )

        def unfold_and_deal(dealt_bytes, folded):
            nc.vector.tensor_copy(folded[P // 2 : P, 0:ROW_WORDS], folded[0 : P // 2, ROW_WORDS : 2 * ROW_WORDS])
            deal(nc.vector.tensor_copy, dealt_bytes[:], folded[:, 0:ROW_WORDS].bitcast(U8), 1)

        def half(h):
            return slice(h * HALF, (h + 1) * HALF), slice(h * LIST_COLS, (h + 1) * LIST_COLS)

        w2_folded = zeroed_folded("w2_folded")
        xo_plane = zeroed_plane("xo_plane", Z)
        w_folded = zeroed_folded("w_folded")
        xt_plane = zeroed_plane("xt_plane", T)
        wb_plane = zeroed_plane("wb_plane", N)
        ws_plane = zeroed_plane("ws_plane", N)

        list2 = load_list("list2", offs2)
        xo_table = load_words("xo_table", xo_words, Z, U16)
        load_folded(w2_folded, w2_scales)
        load_plane(xo_plane, xo_scales)
        w2_natural = load_words("w2_natural", w2_words, R, U32)
        load_folded(w_folded, w_scales)
        w_natural = load_words("w_natural", w_words, R, U16)
        xt_table = load_words("xt_table", xt_words, T, U32)
        load_plane(xt_plane, xt_scales)
        list1 = load_list("list1", offs)
        list4 = load_list("list4", offs4)
        list5 = load_list("list5", offs5)
        list3 = load_list("list3", offs3)
        list6 = load_list("list6", offs6)
        wb_codes = load_words("wb_codes", wb_words, N, U32)
        load_plane(wb_plane, wb_scales)
        ws_codes = load_words("ws_codes", ws_words, N, U32)
        load_plane(ws_plane, ws_scales)

        pages = [sbuf("page%d" % n, [P, E], F32) for n in range(N // P)]
        for page in pages:
            nc.vector.memset(page[:], 0.0)

        xo_codes = sbuf("xo_codes", [P, J], U16)
        xo_bytes = sbuf("xo_bytes", [P, J], U8)
        w2_codes = sbuf("w2_codes", [P, PACK, P], U32)
        w2_bytes = sbuf("w2_bytes", [P, PACK, P], U8)
        w_codes = sbuf("w_codes", [P, PACK, P], U16)
        w_bytes = sbuf("w_bytes", [P, PACK, P], U8)
        nc.vector.tensor_copy(xo_codes[:], xo_table[:].indirect(list2[:]))
        unfold_and_deal(w2_bytes, w2_folded)
        nc.vector.tensor_copy(xo_bytes[:], xo_plane[:].indirect(list2[:]))
        unfold_and_deal(w_bytes, w_folded)
        deal(nc.scalar.copy, w2_codes[:], w2_natural[:], 4)
        deal(nc.scalar.copy, w_codes[:], w_natural[:], 2)

        b_rows = []
        for t in range(PACK):
            bank = ps.tile([P, J], F32, name="b_bank%d" % t, tag="reused%d" % t)
            nc.tensor.matmul_mx(
                out=bank[:], lhsT=w2_codes[:, t, :].bitcast(E5M2), lhsT_scale=w2_bytes[:, t, :],
                rhs=xo_codes[:].bitcast(E2M1), rhs_scale=xo_bytes[:], start=True, stop=True,
            )
            rows = sbuf("b_rows%d" % t, [P, J], F32)
            nc.scalar.copy(rows[:], bank[:])
            b_rows.append(rows)

        xt_codes = sbuf("xt_codes", [P, J], U32)
        xt_bytes = sbuf("xt_bytes", [P, J], U8)
        a_rows = [sbuf("a_rows%d" % t, [P, J], F32) for t in range(PACK)]
        a_banks = []
        for h in range(J // HALF):
            cols, entries = half(h)
            nc.vector.tensor_copy(xt_codes[:, cols], xt_table[:].indirect(list1[:, entries]))
            nc.vector.tensor_copy(xt_bytes[:, cols], xt_plane[:].indirect(list1[:, entries]))
            banks = [ps.tile([P, 2, HALF], F32, name="a_bank%d_%d" % (h, u)) for u in range(PACK // 2)]
            for t in range(PACK):
                nc.tensor.matmul_mx(
                    out=banks[t // 2][:, t % 2, :], lhsT=w_codes[:, t, :].bitcast(E2M1), lhsT_scale=w_bytes[:, t, :],
                    rhs=xt_codes[:, cols].bitcast(E4M3), rhs_scale=xt_bytes[:, cols], start=True, stop=True,
                )
            a_banks.append(banks)
        for h in range(J // HALF):
            for t in range(PACK):
                nc.vector.tensor_copy(a_rows[t][:, half(h)[0]], a_banks[h][t // 2][:, t % 2, :])

        short_codes = sbuf("short_codes", [P, D], U32)
        short_bytes = sbuf("short_bytes", [P, D], U8)
        picks = {1: (b_rows, list4, a_rows), 0: (a_rows, list3, b_rows)}
        for step, h in enumerate((1, 0)):
            cols, entries = half(h)
            source, places, partner = picks[h]

            picked = sbuf("picked%d" % h, [P, PACK, HALF], BF16)
            for t in range(PACK):
                nc.scalar.activation(picked[:, t, :], source[t][:].indirect(places[:]), COPY, scale=partner[t][:, 0:1])
            nc.vector.tensor_copy(short_codes[:, cols], xt_table[:].indirect(list5[:, entries]))
            nc.vector.tensor_copy(short_bytes[:, cols], xt_plane[:].indirect(list5[:, entries]))

            woven = sbuf("woven%d" % h, [P, HALF, PACK], BF16)
            nc.vector.tensor_copy(
                woven[:].rearrange("p (c i) t -> p c t i", i=4), picked[:].rearrange("p t (c i) -> p c t i", i=4)
            )
            hid_codes = sbuf("hid_codes%d" % h, [P, HALF], U32)
            hid_bytes = sbuf("hid_bytes%d" % h, [P, HALF], U8)
            nc.vector.quantize_mx(
                out=hid_codes[:].bitcast(E4M3), scales=hid_bytes[:], in_=woven[:].rearrange("p d t -> p (d t)")
            )

            for n in (h, 1 - h):
                out_rows = slice(n * P, (n + 1) * P)
                bank = ps.tile([P, HALF], F32, name="p_bank%d_%d" % (h, n), tag="reused%d" % (2 * step + n))
                nc.tensor.matmul_mx(
                    out=bank[:], lhsT=ws_codes[:, out_rows].bitcast(E5M2), lhsT_scale=ws_plane[:, out_rows],
                    rhs=short_codes[:, cols].bitcast(E4M3), rhs_scale=short_bytes[:, cols], start=True, stop=False,
                )
                nc.tensor.matmul_mx(
                    out=bank[:], lhsT=wb_codes[:, out_rows].bitcast(E5M2), lhsT_scale=wb_plane[:, out_rows],
                    rhs=hid_codes[:].bitcast(E4M3), rhs_scale=hid_bytes[:], start=False, stop=True,
                )
                target = pages[n][:].indirect(list6[:, entries])
                if n == 0:
                    sums = sbuf("sums0", [P, HALF], F32)
                    nc.scalar.copy(sums[:], bank[:])
                    nc.scalar.activation(target, sums[:], COPY)
                else:
                    sums = sbuf("sums1_%d" % h, [P, HALF], F32)
                    empty = nc.scalar.copy if step == 0 else nc.vector.tensor_copy
                    empty(sums[:], bank[:])
                    nc.vector.tensor_copy(target, sums[:])

        nc.scalar.dma_start(out[0:P, :], pages[0][:])
        nc.sync.dma_start(out[P : 2 * P, :], pages[1][:])
